import numpy as np
import ml_dtypes


def mxq(x, axis, fmt="e4m3"):
    dtype, down = {"e4m3": (ml_dtypes.float8_e4m3fn, 7), "e5m2": (ml_dtypes.float8_e5m2, 14)}[fmt]
    v = np.moveaxis(np.asarray(x, np.float32).astype(ml_dtypes.bfloat16).astype(np.float64), axis, -1)
    blocks = v.reshape(v.shape[:-1] + (-1, 32))
    amax = np.abs(blocks).max(-1, keepdims=True)
    byte = np.maximum(np.where(amax > 0, np.frexp(amax)[1] - 1 + 127, 0) - down, 1)
    scale = np.exp2(byte - 127.0)
    codes = (blocks / scale).astype(np.float32).astype(dtype).astype(np.float64)
    return np.moveaxis((codes * scale).reshape(v.shape), -1, axis)


WIDE = False


def mx_kscale(k):
    if not WIDE:
        return np.ones(k)
    levels = np.array([10, -10, 5, -5, 0])
    if k % 512:
        return np.exp2(np.random.permutation(np.resize(levels, k // 32))).repeat(32)
    a = np.empty((k // 512, 16))
    for p in range(k // 512):
        a[p, :8] = np.random.permutation(np.resize(levels, 8))
        for g in range(8):
            far = levels[np.abs(levels - a[p, g]) >= 10]
            a[p, g + 8] = far[np.random.randint(len(far))]
    return np.exp2(a.ravel()).repeat(32)


def f64(x):
    return np.asarray(x).astype(np.float64)


def striped(idx):
    return np.tile(idx.reshape(-1, 16).T, (8, 1)).astype(np.uint16)


def unstriped(offs):
    return offs[:16].T.reshape(-1).astype(np.int64)


E2M1 = np.array([0.0, 0.5, 1.0, 1.5, 2.0, 3.0, 4.0, 6.0, -0.0, -0.5, -1.0, -1.5, -2.0, -3.0, -4.0, -6.0])


def pack_weight(w, fmt):
    k, n = w.shape
    w = f64(np.asarray(w, np.float32).astype(ml_dtypes.bfloat16)).reshape(k // 32, 32, n)
    amax = np.abs(w).max(1)
    if fmt == "e4m3":
        byte = np.frexp(amax)[1] - 1 + 127 - 7
    else:
        mant, ex = np.frexp(amax / 6.0)
        byte = np.where(mant > 0.5, ex, ex - 1) + 127
    byte = np.clip(np.where(amax > 0, byte, 1), 1, 254)
    scaled = (w * np.exp2(127.0 - byte)[:, None, :]).reshape(k, n).astype(np.float32)
    by_word = np.ascontiguousarray(scaled.reshape(k // 512, 128, 4, n).transpose(0, 1, 3, 2))
    if fmt == "e4m3":
        words = by_word.astype(ml_dtypes.float8_e4m3fn).view(np.uint8)
    else:
        c = by_word.astype(ml_dtypes.float4_e2m1fn).view(np.uint8) & 0xF
        words = (c[..., 0::2] | (c[..., 1::2] << 4)).reshape(k // 512, 128, 2 * n)
    return np.ascontiguousarray(words), np.ascontiguousarray(byte.astype(np.uint8).reshape(k // 512, 16, n))


def unpack_weight(words, scales, fmt):
    g, _, n = scales.shape
    words = np.ascontiguousarray(words).reshape(g, 128, n, -1)
    if fmt == "e4m3":
        vals = words.view(ml_dtypes.float8_e4m3fn).astype(np.float64)
    else:
        nib = np.empty((g, 128, n, 4), np.uint8)
        nib[..., 0::2] = words & 0xF
        nib[..., 1::2] = words >> 4
        vals = E2M1[nib]
    vals = vals * np.repeat(np.exp2(scales.astype(np.float64) - 127.0), 8, axis=1)[..., None]
    return vals.transpose(0, 1, 3, 2).reshape(g * 512, n)


def gelu(v):
    return 0.5 * v * (1.0 + np.tanh(np.sqrt(2.0 / np.pi) * (v + 0.044715 * v**3)))


K, T, S, T2, P, H, N = 1024, 4096, 1024, 2048, 1024, 512, 512

def setup_inputs():
    n = np.random.standard_normal
    s = mx_kscale(K)[:, None]
    u = mx_kscale(H)[:, None]
    tab_words, tab_scales = pack_weight(n((K, T)) * s, "e4m3")
    w1_words, w1_scales = pack_weight(n((K, H)) / np.sqrt(K) / s, "e2m1")
    w2 = (n((K, H)) / np.sqrt(K) / s).astype(np.float32)
    w3_words, w3_scales = pack_weight(n((K, H)) / np.sqrt(K) / s, "e4m3")
    page0 = (0.8 * n((H, T2))).astype(np.float32)
    wgs = np.exp(0.3 * n((128, S))).astype(np.float32)
    thr = n(H).astype(np.float32)
    gain = (np.random.choice([-1.0, 1.0], H) * np.random.uniform(1.2, 2.4, H) * u[:, 0]).astype(np.float32)
    remarks = (0.5 * n((H, P)) * u).astype(np.float32)
    w4 = (n((H, N)) / np.sqrt(H) / u).astype(np.float32)
    offs = striped(np.random.permutation(T)[:S])
    offs2 = striped(np.random.permutation(T2)[:S])
    offs3 = striped(np.random.permutation(T2)[:P])
    return {"tab_words": tab_words, "tab_scales": tab_scales, "offs": offs, "offs2": offs2, "offs3": offs3,
            "w1_words": w1_words, "w1_scales": w1_scales, "w2": w2, "w3_words": w3_words, "w3_scales": w3_scales,
            "page0": page0, "wgs": wgs, "thr": thr, "gain": gain, "remarks": remarks, "w4": w4}

def reference(tab_words, tab_scales, offs, offs2, offs3, w1_words, w1_scales, w2, w3_words, w3_scales,
              page0, wgs, thr, gain, remarks, w4):
    v = unpack_weight(tab_words, tab_scales, "e4m3")[:, unstriped(offs)]
    load = unpack_weight(w1_words, w1_scales, "e2m1").T @ v
    wear = mxq(f64(w2), 0, "e4m3").T @ v
    limit = unpack_weight(w3_words, w3_scales, "e4m3").T @ v
    h = np.minimum(np.maximum(load, wear), limit)
    page = f64(page0).copy()
    page[:, unstriped(offs2)] = np.tile(f64(wgs), (H // 128, 1)) * h
    a = 1.0 / (1.0 + np.exp(-(page[:, unstriped(offs3)] + f64(thr)[:, None])))
    y = f64(gain)[:, None] * a + f64(remarks)
    return mxq(f64(w4), 0, "e4m3").T @ mxq(y, 0, "e4m3")

@@ -1,0 +1,290 @@
+from contextlib import ExitStack
+
+import concourse.mybir as mybir
+
+K, T, S, T2, PM, H, N = 1024, 4096, 1024, 2048, 1024, 512, 512
+FLOPS = 2 * (3 * K * H * S + H * N * PM)
+
+F32 = mybir.dt.float32
+BF16 = mybir.dt.bfloat16
+I32 = mybir.dt.int32
+U32 = mybir.dt.uint32
+U16 = mybir.dt.uint16
+U8 = mybir.dt.uint8
+FP8X4 = mybir.dt.float8_e4m3fn_x4
+FP4X4 = mybir.dt.float4_e2m1fn_x4
+ALU = mybir.AluOpType
+ACT = mybir.ActivationFunctionType
+
+P = 128
+PACK = 4
+PASSES = K // (P * PACK)
+QUADS = 4
+BANK = 512
+HALVES = S // BANK
+STEPS = PACK * HALVES
+LIST_COLS = BANK // 16
+ROW0 = 96
+AREA_TAB0, AREA_TAB1, AREA_W2, AREA_ROWS, AREA_FIRST, AREA_REST0, AREA_REST1 = 0, 20, 36, 52, 54, 62, 70
+WGS_CUTS = (0, BANK, 4 * BANK, 8 * BANK)
+WIDTHS = (256, 256, 256, 128, 128)
+
+
+def tile_list_hoist_caution_scores_kernel(
+    tc, tab_words, tab_scales, offs, offs2, offs3, w1_words, w1_scales, w2, w3_words, w3_scales,
+    page0, wgs, thr, gain, remarks, w4, out,
+):
+    nc = tc.nc
+    with ExitStack() as ctx:
+        keep = ctx.enter_context(tc.tile_pool(name="keep", bufs=1))
+        ring = ctx.enter_context(tc.tile_pool(name="ring", bufs=2))
+        psum = ctx.enter_context(tc.psum_pool(name="psum", bufs=1))
+
+        shared = ctx.enter_context(tc.tile_pool(name="shared", bufs=1))
+
+        def slot(kib, shape, dtype, name):
+            return shared.tile(shape, dtype, name=name, align_bytes=64, offset=1024 * kib)
+
+        def bank(b, shape):
+            return psum.tile(shape, F32, name="bank%d" % b, tag="bank%d" % b)
+
+        idx = keep.tile([P, S // 16], U16, name="idx")
+        idx2 = keep.tile([P, S // 16], U16, name="idx2")
+        idx3 = keep.tile([P, PM // 16], U16, name="idx3")
+        tabw = [slot((AREA_TAB0, AREA_TAB1)[a], [P, T], I32, "tabw%d" % a) for a in range(PASSES)]
+        tabs = keep.tile([P, T], U8, name="tabs")
+        ws_raw = keep.tile([P, 2, H], U8, name="ws_raw")
+        planes = keep.tile([P, PASSES, S + 2 * H], U8, name="planes", align_bytes=64)
+        nc.vector.memset(tabs[0:ROW0, :].bitcast(I32), 0)
+        nc.vector.memset(ws_raw[0:ROW0, :, :].bitcast(I32), 0)
+        nc.gpsimd.memset(planes[:].bitcast(I32), 0)
+
+        nc.sync.dma_start(tabs[ROW0:P, :].bitcast(I32), tab_scales.rearrange("a q t -> q a t").bitcast(I32))
+        nc.sync.dma_start(idx[:], offs)
+        for w, scales in enumerate((w1_scales, w3_scales)):
+            nc.sync.dma_start(ws_raw[ROW0:P, w, :].bitcast(I32), scales.rearrange("a q c -> q a c").bitcast(I32))
+        nc.sync.dma_start(tabw[0][:], tab_words[0].rearrange("p t i -> p (t i)").bitcast(I32))
+        nc.sync.dma_start(idx2[:], offs2)
+        nc.sync.dma_start(idx3[:], offs3)
+        w1_raw = keep.tile([P, PASSES, 2 * H], U8, name="w1_raw")
+        nc.sync.dma_start(w1_raw[:].bitcast(I32), w1_words.rearrange("a p c -> p a c").bitcast(I32))
+        nc.sync.dma_start(tabw[1][:], tab_words[1].rearrange("p t i -> p (t i)").bitcast(I32))
+
+        vs_picked = slot(AREA_W2, [P, S], U8, "vs_picked")
+        nc.vector.tensor_copy(vs_picked[:], tabs[:].indirect(idx[:]))
+
+        def deal(dst, src, run):
+            nc.vector.tensor_copy(dst.rearrange("p a (t c i) -> p a c t i", t=PACK, i=run),
+                                  src.rearrange("p a (c i t) -> p a c t i", t=PACK, i=run))
+
+        rows = slot(AREA_ROWS, [P, S + 2 * H], U8, "rows")
+        deal(rows[:, S:].rearrange("p (w c) -> p w c", w=2), ws_raw[:], 16)
+        nc.vector.tensor_copy(rows[:, 0:S].bitcast(I32), vs_picked[:].bitcast(I32))
+        for q in range(QUADS):
+            nc.sync.dma_start(planes[32 * q : 32 * q + 4, :, :].bitcast(I32),
+                              rows[ROW0 + 8 * q : ROW0 + 8 * (q + 1), :].bitcast(I32))
+        w2_raw = slot(AREA_W2, [P, PASSES, PACK, H], F32, "w2_raw")
+        for a in range(PASSES):
+            nc.sync.dma_start(w2_raw[:, a], w2[512 * a : 512 * (a + 1), :].rearrange("(p j) c -> p j c", j=PACK))
+
+        vw = [keep.tile([P, S], U32, name="vw%d" % a, align_bytes=64) for a in range(PASSES)]
+        nc.vector.tensor_copy(vw[0][:], tabw[0][:].bitcast(U32).indirect(idx[:]))
+        page_rows = page0.rearrange("(p t) c -> p t c", t=PACK)
+        page = {}
+
+        def load_page(t, kib):
+            page[t] = slot(kib, [P, T2], F32, "page%d" % t)
+            nc.sync.dma_start(page[t][:], page_rows[:, t, :])
+
+        w3_raw = slot(AREA_TAB0 + 12, [P, PASSES, H], I32, "w3_raw")
+        nc.sync.dma_start(w3_raw[:], w3_words.rearrange("a p c i -> p a (c i)").bitcast(I32))
+        load_page(0, AREA_TAB0)
+        thr_sb = slot(AREA_TAB0 + 8, [P, PACK], F32, "thr_sb")
+        nc.sync.dma_start(thr_sb[:], thr.rearrange("(p t) -> p t", t=PACK))
+        gain_sb = slot(AREA_TAB0 + 9, [P, PACK], F32, "gain_sb")
+        nc.sync.dma_start(gain_sb[:], gain.rearrange("(p t) -> p t", t=PACK))
+        wgs_rows = wgs.rearrange("(q t) j -> q (t j)", t=PACK)
+        wgs_parts = {}
+
+        def load_wgs(part, kib):
+            lo, hi = WGS_CUTS[part], WGS_CUTS[part + 1]
+            dealt = slot(kib, [P, hi - lo], F32, "wgs%d" % part)
+            for q in range(QUADS):
+                nc.sync.dma_start(dealt[32 * q : 32 * (q + 1), :], wgs_rows[:, lo:hi])
+            for n in range(lo // BANK, hi // BANK):
+                wgs_parts[n] = dealt[:, BANK * n - lo : BANK * (n + 1) - lo]
+
+        load_wgs(0, AREA_ROWS)
+
+        w1c = keep.tile([P, PASSES, 2 * H], U8, name="w1c", align_bytes=64)
+        w3c = keep.tile([P, PASSES, H], I32, name="w3c", align_bytes=64)
+        deal(w1c[:].bitcast(U16), w1_raw[:].bitcast(U16), 8)
+
+        for u in range(HALVES):
+            nc.vector.tensor_copy(vw[1][:, BANK * u : BANK * (u + 1)],
+                                  tabw[1][:].bitcast(U32).indirect(idx[:, LIST_COLS * u : LIST_COLS * (u + 1)]))
+
+        load_wgs(1, AREA_TAB1)
+        load_page(1, AREA_TAB1 + 6)
+
+        w2_codes, w2_scales, w2_rest_bf = {}, {}, {}
+        for a in range(PASSES):
+            first_bf = slot(AREA_FIRST + a, [P, P, PACK], BF16, "w2_first_bf%d" % a)
+            nc.vector.tensor_copy(first_bf[:], w2_raw[:, a].rearrange("p j (m t) -> p t m j", t=PACK)[:, 0, :, :])
+            codes = keep.tile([P, P], U32, name="w2_first_codes%d" % a, align_bytes=64)
+            scales = keep.tile([P, P], U8, name="w2_first_scales%d" % a, align_bytes=64)
+            nc.vector.quantize_mx(out=codes[:].bitcast(FP8X4), scales=scales[:],
+                                  in_=first_bf[:].rearrange("p m j -> p (m j)"))
+            w2_codes[a, 0], w2_scales[a, 0] = codes[:], scales[:]
+        deal(w3c[:], w3_raw[:], 4)
+        load_page(2, AREA_TAB0 + 12)
+        load_wgs(2, AREA_FIRST)
+
+        def round_w2_rest(a):
+            rest_bf = slot((AREA_REST0, AREA_REST1)[a], [P, PACK - 1, P, PACK], BF16, "w2_rest_bf%d" % a)
+            nc.scalar.copy(rest_bf[:].rearrange("p t m j -> p m j t"),
+                           w2_raw[:, a].rearrange("p j (m t) -> p m j t", t=PACK)[:, :, :, 1:PACK])
+            w2_rest_bf[a] = rest_bf
+
+        def quantise_w2_rest(a):
+            codes = keep.tile([P, (PACK - 1) * P], U32, name="w2_rest_codes%d" % a, align_bytes=64)
+            scales = keep.tile([P, (PACK - 1) * P], U8, name="w2_rest_scales%d" % a, align_bytes=64)
+            nc.vector.quantize_mx(out=codes[:].bitcast(FP8X4), scales=scales[:],
+                                  in_=w2_rest_bf[a][:].rearrange("p t m j -> p (t m j)"))
+            for t in range(1, PACK):
+                w2_codes[a, t] = codes[:, P * (t - 1) : P * t]
+                w2_scales[a, t] = scales[:, P * (t - 1) : P * t]
+
+        def product(b, n, operand):
+            t, u = divmod(n, HALVES)
+            cols = slice(BANK * u, BANK * (u + 1))
+            acc = bank(b, [P, BANK])
+            for a in range(PASSES):
+                codes, scales = operand(a, t)
+                nc.tensor.matmul_mx(out=acc[:], lhsT=codes, lhsT_scale=scales,
+                                    rhs=vw[a][:, cols].bitcast(FP8X4), rhs_scale=planes[:, a, cols],
+                                    start=(a == 0), stop=(a == PASSES - 1))
+            return acc
+
+        def w1_operand(a, t):
+            return w1c[:, a, 2 * P * t : 2 * P * (t + 1)].bitcast(FP4X4), planes[:, a, S + P * t : S + P * (t + 1)]
+
+        def w2_operand(a, t):
+            return w2_codes[a, t].bitcast(FP8X4), w2_scales[a, t]
+
+        def w3_operand(a, t):
+            return w3c[:, a, P * t : P * (t + 1)].bitcast(FP8X4), planes[:, a, S + H + P * t : S + H + P * (t + 1)]
+
+        load_sb, wear, limit, worse = {}, {}, {}, {}
+
+        def load_product(n):
+            acc = product(n % 2, n, w1_operand)
+            load_sb[n] = ring.tile([P, BANK], F32, name="load_sb", tag="load_sb", bufs=STEPS)
+            nc.scalar.copy(load_sb[n][:], acc[:])
+
+        def limit_product(n):
+            limit[n] = product(5 + n % 3, n, w3_operand)
+
+        def wear_product(n):
+            wear[n] = product(2 + n % 3, n, w2_operand)
+
+        def take_max(n):
+            worse[n] = ring.tile([P, BANK], F32, name="worse", tag="worse")
+            nc.vector.tensor_tensor(worse[n][:], wear[n][:], load_sb[n][:], ALU.max)
+
+        looked = keep.tile([P, PACK, PM], F32, name="looked")
+        gained = keep.tile([P, PACK, PM], F32, name="gained")
+
+        def look(t, lo, hi):
+            nc.scalar.activation(out=looked[:, t, lo:hi], in_=page[t][:].indirect(idx3[:, lo // 16 : hi // 16]),
+                                 func=ACT.Sigmoid, bias=thr_sb[:, t : t + 1])
+
+        def apply_gain(t, lo, hi):
+            nc.scalar.activation(out=gained[:, t, lo:hi], in_=looked[:, t, lo:hi], func=ACT.Copy,
+                                 scale=gain_sb[:, t : t + 1])
+
+        round_w2_rest(0)
+        for n in range(2):
+            load_product(n)
+        for n in range(2):
+            wear_product(n)
+            limit_product(n)
+        round_w2_rest(1)
+        rem = slot(AREA_W2, [P, PACK, PM], F32, "rem")
+        nc.sync.dma_start(rem[:], remarks.rearrange("(p t) m -> p t m", t=PACK))
+        take_max(0)
+        w4_bf = keep.tile([P, N, PACK], BF16, name="w4_bf", align_bytes=64)
+        for n in range(STEPS):
+            t, u = divmod(n, HALVES)
+            h = ring.tile([P, BANK], F32, name="h", tag="h")
+            nc.vector.tensor_tensor(h[:], limit[n][:], worse[n][:], ALU.min)
+            if n + 1 < STEPS:
+                take_max(n + 1)
+            nc.vector.tensor_tensor(page[t][:].indirect(idx2[:, LIST_COLS * u : LIST_COLS * (u + 1)]),
+                                    h[:], wgs_parts[n], ALU.mult)
+            if n == 0:
+                for a in range(PASSES):
+                    quantise_w2_rest(a)
+                w4_raw = slot(AREA_REST0, [P, PACK, N], F32, "w4_raw")
+                nc.sync.dma_start(w4_raw[:], w4.rearrange("(p j) n -> p j n", j=PACK))
+                load_page(3, AREA_REST1)
+            if n + 2 < STEPS:
+                load_product(n + 2)
+                wear_product(n + 2)
+                limit_product(n + 2)
+            if u == HALVES - 1 and t < PACK - 1:
+                look(t, 0, PM)
+                apply_gain(t, 0, PM)
+            if n == STEPS - 3:
+                nc.scalar.copy(w4_bf[:].rearrange("p (c i) j -> p c j i", i=4),
+                               w4_raw[:].rearrange("p j (c i) -> p c j i", i=4))
+
+        w4_codes = slot(AREA_FIRST + 6, [P, N], U32, "w4_codes")
+        w4_scales = keep.tile([P, N], U8, name="w4_scales", align_bytes=64)
+        nc.vector.quantize_mx(out=w4_codes[:].bitcast(FP8X4), scales=w4_scales[:],
+                              in_=w4_bf[:].rearrange("p n j -> p (n j)"))
+
+        chunks = len(WIDTHS)
+        starts = [sum(WIDTHS[:c]) for c in range(chunks + 1)]
+        out_rows = out.rearrange("(b p) m -> p b m", p=P)
+        y_bf = {}
+
+        def add_remarks(c):
+            cols = slice(starts[c], starts[c + 1])
+            y_bf[c] = keep.tile([P, WIDTHS[c], PACK], BF16, name="y_bf%d" % c, align_bytes=64)
+            nc.vector.tensor_tensor(y_bf[c][:].rearrange("p (c i) t -> p c t i", i=2),
+                                    gained[:, :, cols].rearrange("p t (c i) -> p c t i", i=2),
+                                    rem[:, :, cols].rearrange("p t (c i) -> p c t i", i=2), ALU.add)
+
+        def finish(c):
+            cols = slice(starts[c], starts[c + 1])
+            width = WIDTHS[c]
+            codes = keep.tile([P, width], U32, name="y_codes%d" % c, align_bytes=64)
+            scales = keep.tile([P, width], U8, name="y_scales%d" % c, align_bytes=64)
+            nc.vector.quantize_mx(out=codes[:].bitcast(FP8X4), scales=scales[:],
+                                  in_=y_bf[c][:].rearrange("p m t -> p (m t)"))
+            for g in range(2):
+                acc = bank((2 * c + g) % 8, [P, 2, width])
+                for e in range(2):
+                    ncols = slice(P * (2 * g + e), P * (2 * g + e + 1))
+                    nc.tensor.matmul_mx(out=acc[:, e, :], lhsT=w4_codes[:, ncols].bitcast(FP8X4),
+                                        lhsT_scale=w4_scales[:, ncols], rhs=codes[:].bitcast(FP8X4),
+                                        rhs_scale=scales[:], start=True, stop=True)
+                staged = keep.tile([P, 2, width], F32, name="staged%d_%d" % (c, g))
+                if c == chunks - 1 and g == 1:
+                    nc.vector.tensor_copy(staged[:], acc[:])
+                else:
+                    nc.scalar.copy(staged[:], acc[:])
+                nc.sync.dma_start(out_rows[:, 2 * g : 2 * g + 2, cols], staged[:])
+
+        last = PACK - 1
+        for u in range(HALVES):
+            look(last, BANK * u, BANK * (u + 1))
+            for c in range(chunks):
+                if starts[c] // BANK == u:
+                    apply_gain(last, starts[c], starts[c + 1])
+        for c in range(chunks):
+            add_remarks(c)
+            if c > 0:
+                finish(c - 1)
+        finish(chunks - 1)

@@ -25,7 +25,8 @@ HALVES = S // BANK
 STEPS = PACK * HALVES
 LIST_COLS = BANK // 16
 ROW0 = 96
-AREA_TAB0, AREA_TAB1, AREA_W2, AREA_ROWS, AREA_FIRST, AREA_REST0, AREA_REST1 = 0, 20, 36, 52, 54, 62, 70
+AREA_TAB0, AREA_TAB1, AREA_W2, AREA_ROWS, AREA_FIRST, AREA_W4 = 0, 23, 39, 55, 64, 73
+AREA_LOAD = 81
 WGS_CUTS = (0, BANK, 4 * BANK, 8 * BANK)
 WIDTHS = (256, 256, 256, 128, 128)
 
@@ -109,10 +110,10 @@ def tile_list_hoist_caution_scores_kernel(
         def load_wgs(part, kib):
             lo, hi = WGS_CUTS[part], WGS_CUTS[part + 1]
             dealt = slot(kib, [P, hi - lo], F32, "wgs%d" % part)
-            for q in range(QUADS):
+            for q in (0, 2, 1, 3):
                 nc.sync.dma_start(dealt[32 * q : 32 * (q + 1), :], wgs_rows[:, lo:hi])
             for n in range(lo // BANK, hi // BANK):
-                wgs_parts[n] = dealt[:, BANK * n - lo : BANK * (n + 1) - lo]
+                wgs_parts[n] = (dealt, lo)
 
         load_wgs(0, AREA_ROWS)
 
@@ -127,7 +128,7 @@ def tile_list_hoist_caution_scores_kernel(
         load_wgs(1, AREA_TAB1)
         load_page(1, AREA_TAB1 + 6)
 
-        w2_codes, w2_scales, w2_rest_bf = {}, {}, {}
+        w2_codes, w2_scales, w2_bf = {}, {}, {}
         for a in range(PASSES):
             first_bf = slot(AREA_FIRST + a, [P, P, PACK], BF16, "w2_first_bf%d" % a)
             nc.vector.tensor_copy(first_bf[:], w2_raw[:, a].rearrange("p j (m t) -> p t m j", t=PACK)[:, 0, :, :])
@@ -137,23 +138,21 @@ def tile_list_hoist_caution_scores_kernel(
                                   in_=first_bf[:].rearrange("p m j -> p (m j)"))
             w2_codes[a, 0], w2_scales[a, 0] = codes[:], scales[:]
         deal(w3c[:], w3_raw[:], 4)
-        load_page(2, AREA_TAB0 + 12)
-        load_wgs(2, AREA_FIRST)
+        load_wgs(2, AREA_FIRST + 1)
 
-        def round_w2_rest(a):
-            rest_bf = slot((AREA_REST0, AREA_REST1)[a], [P, PACK - 1, P, PACK], BF16, "w2_rest_bf%d" % a)
-            nc.scalar.copy(rest_bf[:].rearrange("p t m j -> p m j t"),
-                           w2_raw[:, a].rearrange("p j (m t) -> p m j t", t=PACK)[:, :, :, 1:PACK])
-            w2_rest_bf[a] = rest_bf
+        def round_w2(t):
+            w2_bf[t] = slot(AREA_TAB0 + 9 + 2 * t, [P, PASSES, P, PACK], BF16, "w2_bf%d" % t)
+            for a in range(PASSES):
+                nc.scalar.copy(w2_bf[t][:, a], w2_raw[:, a].rearrange("p j (m t) -> p t m j", t=PACK)[:, t, :, :])
 
-        def quantise_w2_rest(a):
-            codes = keep.tile([P, (PACK - 1) * P], U32, name="w2_rest_codes%d" % a, align_bytes=64)
-            scales = keep.tile([P, (PACK - 1) * P], U8, name="w2_rest_scales%d" % a, align_bytes=64)
-            nc.vector.quantize_mx(out=codes[:].bitcast(FP8X4), scales=scales[:],
-                                  in_=w2_rest_bf[a][:].rearrange("p t m j -> p (t m j)"))
-            for t in range(1, PACK):
-                w2_codes[a, t] = codes[:, P * (t - 1) : P * t]
-                w2_scales[a, t] = scales[:, P * (t - 1) : P * t]
+        def quantise_w2(t):
+            codes = slot((AREA_ROWS, AREA_LOAD + 4, AREA_LOAD + 8)[t - 1], [P, PASSES, P], U32, "w2_codes%d" % t)
+            scales = keep.tile([P, PASSES, P], U8, name="w2_scales%d" % t, align_bytes=64)
+            nc.vector.quantize_mx(out=codes[:].rearrange("p a m -> p (a m)").bitcast(FP8X4),
+                                  scales=scales[:].rearrange("p a m -> p (a m)"),
+                                  in_=w2_bf[t][:].rearrange("p a m j -> p (a m j)"))
+            for a in range(PASSES):
+                w2_codes[a, t], w2_scales[a, t] = codes[:, a, :], scales[:, a, :]
 
         def product(b, n, operand):
             t, u = divmod(n, HALVES)
@@ -179,7 +178,7 @@ def tile_list_hoist_caution_scores_kernel(
 
         def load_product(n):
             acc = product(n % 2, n, w1_operand)
-            load_sb[n] = ring.tile([P, BANK], F32, name="load_sb", tag="load_sb", bufs=STEPS)
+            load_sb[n] = slot({1: AREA_W4, 3: AREA_FIRST - 7}.get(n, AREA_LOAD + 2 * n), [P, BANK], F32, "load_sb%d" % n)
             nc.scalar.copy(load_sb[n][:], acc[:])
 
         def limit_product(n):
@@ -192,54 +191,68 @@ def tile_list_hoist_caution_scores_kernel(
             worse[n] = ring.tile([P, BANK], F32, name="worse", tag="worse")
             nc.vector.tensor_tensor(worse[n][:], wear[n][:], load_sb[n][:], ALU.max)
 
-        looked = keep.tile([P, PACK, PM], F32, name="looked")
         gained = keep.tile([P, PACK, PM], F32, name="gained")
 
         def look(t, lo, hi):
-            nc.scalar.activation(out=looked[:, t, lo:hi], in_=page[t][:].indirect(idx3[:, lo // 16 : hi // 16]),
+            looked = keep.tile([P, hi - lo], F32, name="looked", tag="looked")
+            nc.scalar.activation(out=looked[:], in_=page[t][:].indirect(idx3[:, lo // 16 : hi // 16]),
                                  func=ACT.Sigmoid, bias=thr_sb[:, t : t + 1])
+            return looked
 
-        def apply_gain(t, lo, hi):
-            nc.scalar.activation(out=gained[:, t, lo:hi], in_=looked[:, t, lo:hi], func=ACT.Copy,
+        def apply_gain(t, looked, base, lo, hi):
+            nc.scalar.activation(out=gained[:, t, lo:hi], in_=looked[:, lo - base : hi - base], func=ACT.Copy,
                                  scale=gain_sb[:, t : t + 1])
 
-        round_w2_rest(0)
+        def put(t, lo, hi):
+            dealt, base = wgs_parts[(S * t + lo) // BANK]
+            nc.vector.tensor_tensor(page[t][:].indirect(idx2[:, lo // 16 : hi // 16]), h[t][:, lo:hi],
+                                    dealt[:, S * t + lo - base : S * t + hi - base], ALU.mult)
+
         for n in range(2):
             load_product(n)
         for n in range(2):
             wear_product(n)
             limit_product(n)
-        round_w2_rest(1)
-        rem = slot(AREA_W2, [P, PACK, PM], F32, "rem")
-        nc.sync.dma_start(rem[:], remarks.rearrange("(p t) m -> p t m", t=PACK))
+        round_w2(1)
+        for n in range(2, STEPS):
+            load_product(n)
         take_max(0)
         w4_bf = keep.tile([P, N, PACK], BF16, name="w4_bf", align_bytes=64)
+        h = {}
         for n in range(STEPS):
             t, u = divmod(n, HALVES)
-            h = ring.tile([P, BANK], F32, name="h", tag="h")
-            nc.vector.tensor_tensor(h[:], limit[n][:], worse[n][:], ALU.min)
+            if u == 0:
+                h[t] = keep.tile([P, S], F32, name="h", tag="h")
+            nc.vector.tensor_tensor(h[t][:, BANK * u : BANK * (u + 1)], limit[n][:], worse[n][:], ALU.min)
             if n + 1 < STEPS:
                 take_max(n + 1)
-            nc.vector.tensor_tensor(page[t][:].indirect(idx2[:, LIST_COLS * u : LIST_COLS * (u + 1)]),
-                                    h[:], wgs_parts[n], ALU.mult)
+            if t == 0:
+                put(t, BANK * u, BANK * (u + 1))
+            elif u == HALVES - 1:
+                put(t, 0, S)
+            if u == 0 and t + 1 < PACK:
+                quantise_w2(t + 1)
+                if t + 2 < PACK:
+                    round_w2(t + 2)
             if n == 0:
-                for a in range(PASSES):
-                    quantise_w2_rest(a)
-                w4_raw = slot(AREA_REST0, [P, PACK, N], F32, "w4_raw")
+                w4_raw = slot(AREA_W4, [P, PACK, N], F32, "w4_raw")
                 nc.sync.dma_start(w4_raw[:], w4.rearrange("(p j) n -> p j n", j=PACK))
-                load_page(3, AREA_REST1)
+            if n == 2:
+                load_page(2, AREA_FIRST - 7)
+            if n == 4:
+                load_page(3, AREA_TAB0 + 15)
+                rem = slot(AREA_W2, [P, PACK, PM], F32, "rem")
+                nc.sync.dma_start(rem[:], remarks.rearrange("(p t) m -> p t m", t=PACK))
             if n + 2 < STEPS:
-                load_product(n + 2)
                 wear_product(n + 2)
                 limit_product(n + 2)
             if u == HALVES - 1 and t < PACK - 1:
-                look(t, 0, PM)
-                apply_gain(t, 0, PM)
+                apply_gain(t, look(t, 0, PM), 0, 0, PM)
             if n == STEPS - 3:
                 nc.scalar.copy(w4_bf[:].rearrange("p (c i) j -> p c j i", i=4),
                                w4_raw[:].rearrange("p j (c i) -> p c j i", i=4))
 
-        w4_codes = slot(AREA_FIRST + 6, [P, N], U32, "w4_codes")
+        w4_codes = slot(AREA_FIRST + 7, [P, N], U32, "w4_codes")
         w4_scales = keep.tile([P, N], U8, name="w4_scales", align_bytes=64)
         nc.vector.quantize_mx(out=w4_codes[:].bitcast(FP8X4), scales=w4_scales[:],
                               in_=w4_bf[:].rearrange("p n j -> p (n j)"))
@@ -279,10 +292,10 @@ def tile_list_hoist_caution_scores_kernel(
 
         last = PACK - 1
         for u in range(HALVES):
-            look(last, BANK * u, BANK * (u + 1))
+            looked = look(last, BANK * u, BANK * (u + 1))
             for c in range(chunks):
                 if starts[c] // BANK == u:
-                    apply_gain(last, starts[c], starts[c + 1])
+                    apply_gain(last, looked, BANK * u, starts[c], starts[c + 1])
         for c in range(chunks):
             add_remarks(c)
             if c > 0:

@@ -25,10 +25,10 @@ HALVES = S // BANK
 STEPS = PACK * HALVES
 LIST_COLS = BANK // 16
 ROW0 = 96
-AREA_TAB0, AREA_TAB1, AREA_W2, AREA_ROWS, AREA_FIRST, AREA_W4 = 0, 23, 39, 55, 64, 73
-AREA_LOAD = 81
+AREA_TAB0, AREA_TAB1, AREA_W2, AREA_ROWS, AREA_FIRST, AREA_REST0, AREA_REST1 = 0, 20, 36, 53, 62, 70, 78
 WGS_CUTS = (0, BANK, 4 * BANK, 8 * BANK)
 WIDTHS = (256, 256, 256, 128, 128)
+GAIN_WIDTHS = (256, 512)
 
 
 def tile_list_hoist_caution_scores_kernel(
@@ -99,11 +99,6 @@ def tile_list_hoist_caution_scores_kernel(
 
         w3_raw = slot(AREA_TAB0 + 12, [P, PASSES, H], I32, "w3_raw")
         nc.sync.dma_start(w3_raw[:], w3_words.rearrange("a p c i -> p a (c i)").bitcast(I32))
-        load_page(0, AREA_TAB0)
-        thr_sb = slot(AREA_TAB0 + 8, [P, PACK], F32, "thr_sb")
-        nc.sync.dma_start(thr_sb[:], thr.rearrange("(p t) -> p t", t=PACK))
-        gain_sb = slot(AREA_TAB0 + 9, [P, PACK], F32, "gain_sb")
-        nc.sync.dma_start(gain_sb[:], gain.rearrange("(p t) -> p t", t=PACK))
         wgs_rows = wgs.rearrange("(q t) j -> q (t j)", t=PACK)
         wgs_parts = {}
 
@@ -113,9 +108,10 @@ def tile_list_hoist_caution_scores_kernel(
             for q in (0, 2, 1, 3):
                 nc.sync.dma_start(dealt[32 * q : 32 * (q + 1), :], wgs_rows[:, lo:hi])
             for n in range(lo // BANK, hi // BANK):
-                wgs_parts[n] = (dealt, lo)
+                wgs_parts[n] = dealt[:, BANK * n - lo : BANK * (n + 1) - lo]
 
-        load_wgs(0, AREA_ROWS)
+        load_wgs(0, AREA_ROWS - 1)
+        load_page(0, AREA_ROWS + 1)
 
         w1c = keep.tile([P, PASSES, 2 * H], U8, name="w1c", align_bytes=64)
         w3c = keep.tile([P, PASSES, H], I32, name="w3c", align_bytes=64)
@@ -127,8 +123,12 @@ def tile_list_hoist_caution_scores_kernel(
 
         load_wgs(1, AREA_TAB1)
         load_page(1, AREA_TAB1 + 6)
+        thr_sb = slot(AREA_TAB1 + 14, [P, PACK], F32, "thr_sb")
+        nc.sync.dma_start(thr_sb[:], thr.rearrange("(p t) -> p t", t=PACK))
+        gain_sb = slot(AREA_TAB1 + 15, [P, PACK], F32, "gain_sb")
+        nc.sync.dma_start(gain_sb[:], gain.rearrange("(p t) -> p t", t=PACK))
 
-        w2_codes, w2_scales, w2_bf = {}, {}, {}
+        w2_codes, w2_scales, w2_rest_bf = {}, {}, {}
         for a in range(PASSES):
             first_bf = slot(AREA_FIRST + a, [P, P, PACK], BF16, "w2_first_bf%d" % a)
             nc.vector.tensor_copy(first_bf[:], w2_raw[:, a].rearrange("p j (m t) -> p t m j", t=PACK)[:, 0, :, :])
@@ -138,21 +138,23 @@ def tile_list_hoist_caution_scores_kernel(
                                   in_=first_bf[:].rearrange("p m j -> p (m j)"))
             w2_codes[a, 0], w2_scales[a, 0] = codes[:], scales[:]
         deal(w3c[:], w3_raw[:], 4)
-        load_wgs(2, AREA_FIRST + 1)
+        load_page(2, AREA_TAB0 + 12)
+        load_wgs(2, AREA_FIRST)
 
-        def round_w2(t):
-            w2_bf[t] = slot(AREA_TAB0 + 9 + 2 * t, [P, PASSES, P, PACK], BF16, "w2_bf%d" % t)
-            for a in range(PASSES):
-                nc.scalar.copy(w2_bf[t][:, a], w2_raw[:, a].rearrange("p j (m t) -> p t m j", t=PACK)[:, t, :, :])
+        def round_w2_rest(a):
+            rest_bf = slot((AREA_REST0, AREA_REST1)[a], [P, PACK - 1, P, PACK], BF16, "w2_rest_bf%d" % a)
+            nc.scalar.copy(rest_bf[:].rearrange("p t m j -> p m j t"),
+                           w2_raw[:, a].rearrange("p j (m t) -> p m j t", t=PACK)[:, :, :, 1:PACK])
+            w2_rest_bf[a] = rest_bf
 
-        def quantise_w2(t):
-            codes = slot((AREA_ROWS, AREA_LOAD + 4, AREA_LOAD + 8)[t - 1], [P, PASSES, P], U32, "w2_codes%d" % t)
-            scales = keep.tile([P, PASSES, P], U8, name="w2_scales%d" % t, align_bytes=64)
-            nc.vector.quantize_mx(out=codes[:].rearrange("p a m -> p (a m)").bitcast(FP8X4),
-                                  scales=scales[:].rearrange("p a m -> p (a m)"),
-                                  in_=w2_bf[t][:].rearrange("p a m j -> p (a m j)"))
-            for a in range(PASSES):
-                w2_codes[a, t], w2_scales[a, t] = codes[:, a, :], scales[:, a, :]
+        def quantise_w2_rest(a):
+            codes = keep.tile([P, (PACK - 1) * P], U32, name="w2_rest_codes%d" % a, align_bytes=64)
+            scales = keep.tile([P, (PACK - 1) * P], U8, name="w2_rest_scales%d" % a, align_bytes=64)
+            nc.vector.quantize_mx(out=codes[:].bitcast(FP8X4), scales=scales[:],
+                                  in_=w2_rest_bf[a][:].rearrange("p t m j -> p (t m j)"))
+            for t in range(1, PACK):
+                w2_codes[a, t] = codes[:, P * (t - 1) : P * t]
+                w2_scales[a, t] = scales[:, P * (t - 1) : P * t]
 
         def product(b, n, operand):
             t, u = divmod(n, HALVES)
@@ -178,7 +180,7 @@ def tile_list_hoist_caution_scores_kernel(
 
         def load_product(n):
             acc = product(n % 2, n, w1_operand)
-            load_sb[n] = slot({1: AREA_W4, 3: AREA_FIRST - 7}.get(n, AREA_LOAD + 2 * n), [P, BANK], F32, "load_sb%d" % n)
+            load_sb[n] = ring.tile([P, BANK], F32, name="load_sb", tag="load_sb", bufs=STEPS)
             nc.scalar.copy(load_sb[n][:], acc[:])
 
         def limit_product(n):
@@ -203,47 +205,33 @@ def tile_list_hoist_caution_scores_kernel(
             nc.scalar.activation(out=gained[:, t, lo:hi], in_=looked[:, lo - base : hi - base], func=ACT.Copy,
                                  scale=gain_sb[:, t : t + 1])
 
-        def put(t, lo, hi):
-            dealt, base = wgs_parts[(S * t + lo) // BANK]
-            nc.vector.tensor_tensor(page[t][:].indirect(idx2[:, lo // 16 : hi // 16]), h[t][:, lo:hi],
-                                    dealt[:, S * t + lo - base : S * t + hi - base], ALU.mult)
-
+        round_w2_rest(0)
         for n in range(2):
             load_product(n)
         for n in range(2):
             wear_product(n)
             limit_product(n)
-        round_w2(1)
-        for n in range(2, STEPS):
-            load_product(n)
+        round_w2_rest(1)
+        rem = slot(AREA_W2, [P, PACK, PM], F32, "rem")
+        nc.sync.dma_start(rem[:], remarks.rearrange("(p t) m -> p t m", t=PACK))
         take_max(0)
         w4_bf = keep.tile([P, N, PACK], BF16, name="w4_bf", align_bytes=64)
-        h = {}
         for n in range(STEPS):
             t, u = divmod(n, HALVES)
-            if u == 0:
-                h[t] = keep.tile([P, S], F32, name="h", tag="h")
-            nc.vector.tensor_tensor(h[t][:, BANK * u : BANK * (u + 1)], limit[n][:], worse[n][:], ALU.min)
+            h = ring.tile([P, BANK], F32, name="h", tag="h")
+            nc.vector.tensor_tensor(h[:], limit[n][:], worse[n][:], ALU.min)
             if n + 1 < STEPS:
                 take_max(n + 1)
-            if t == 0:
-                put(t, BANK * u, BANK * (u + 1))
-            elif u == HALVES - 1:
-                put(t, 0, S)
-            if u == 0 and t + 1 < PACK:
-                quantise_w2(t + 1)
-                if t + 2 < PACK:
-                    round_w2(t + 2)
+            nc.vector.tensor_tensor(page[t][:].indirect(idx2[:, LIST_COLS * u : LIST_COLS * (u + 1)]),
+                                    h[:], wgs_parts[n], ALU.mult)
             if n == 0:
-                w4_raw = slot(AREA_W4, [P, PACK, N], F32, "w4_raw")
+                for a in range(PASSES):
+                    quantise_w2_rest(a)
+                w4_raw = slot(AREA_REST0, [P, PACK, N], F32, "w4_raw")
                 nc.sync.dma_start(w4_raw[:], w4.rearrange("(p j) n -> p j n", j=PACK))
-            if n == 2:
-                load_page(2, AREA_FIRST - 7)
-            if n == 4:
-                load_page(3, AREA_TAB0 + 15)
-                rem = slot(AREA_W2, [P, PACK, PM], F32, "rem")
-                nc.sync.dma_start(rem[:], remarks.rearrange("(p t) m -> p t m", t=PACK))
+                load_page(3, AREA_REST1)
             if n + 2 < STEPS:
+                load_product(n + 2)
                 wear_product(n + 2)
                 limit_product(n + 2)
             if u == HALVES - 1 and t < PACK - 1:
@@ -252,7 +240,7 @@ def tile_list_hoist_caution_scores_kernel(
                 nc.scalar.copy(w4_bf[:].rearrange("p (c i) j -> p c j i", i=4),
                                w4_raw[:].rearrange("p j (c i) -> p c j i", i=4))
 
-        w4_codes = slot(AREA_FIRST + 7, [P, N], U32, "w4_codes")
+        w4_codes = slot(AREA_FIRST + 6, [P, N], U32, "w4_codes")
         w4_scales = keep.tile([P, N], U8, name="w4_scales", align_bytes=64)
         nc.vector.quantize_mx(out=w4_codes[:].bitcast(FP8X4), scales=w4_scales[:],
                               in_=w4_bf[:].rearrange("p n j -> p (n j)"))
@@ -284,18 +272,18 @@ def tile_list_hoist_caution_scores_kernel(
                                         lhsT_scale=w4_scales[:, ncols], rhs=codes[:].bitcast(FP8X4),
                                         rhs_scale=scales[:], start=True, stop=True)
                 staged = keep.tile([P, 2, width], F32, name="staged%d_%d" % (c, g))
-                if c == chunks - 1 and g == 1:
+                if c >= chunks - 2 and g == 1:
                     nc.vector.tensor_copy(staged[:], acc[:])
                 else:
                     nc.scalar.copy(staged[:], acc[:])
-                nc.sync.dma_start(out_rows[:, 2 * g : 2 * g + 2, cols], staged[:])
+                queue = nc.scalar if (c, g) == (chunks - 1, 0) else nc.sync
+                queue.dma_start(out_rows[:, 2 * g : 2 * g + 2, cols], staged[:])
 
         last = PACK - 1
         for u in range(HALVES):
             looked = look(last, BANK * u, BANK * (u + 1))
-            for c in range(chunks):
-                if starts[c] // BANK == u:
-                    apply_gain(last, looked, BANK * u, starts[c], starts[c + 1])
+            for lo in range(BANK * u, BANK * (u + 1), GAIN_WIDTHS[u]):
+                apply_gain(last, looked, BANK * u, lo, lo + GAIN_WIDTHS[u])
         for c in range(chunks):
             add_remarks(c)
             if c > 0:

@@ -25,7 +25,8 @@ HALVES = S // BANK
 STEPS = PACK * HALVES
 LIST_COLS = BANK // 16
 ROW0 = 96
-AREA_TAB0, AREA_TAB1, AREA_W2, AREA_ROWS, AREA_FIRST, AREA_REST0, AREA_REST1 = 0, 20, 36, 53, 62, 70, 78
+QUAD_ORDER = (0, 2, 1, 3)
+AREA_TAB0, AREA_TAB1, AREA_W2, AREA_ROWS, AREA_FIRST0, AREA_FIRST1, AREA_REST0, AREA_REST1 = 0, 20, 36, 54, 69, 78, 86, 94
 WGS_CUTS = (0, BANK, 4 * BANK, 8 * BANK)
 WIDTHS = (256, 256, 256, 128, 128)
 GAIN_WIDTHS = (256, 512)
@@ -44,7 +45,7 @@ def tile_list_hoist_caution_scores_kernel(
         shared = ctx.enter_context(tc.tile_pool(name="shared", bufs=1))
 
         def slot(kib, shape, dtype, name):
-            return shared.tile(shape, dtype, name=name, align_bytes=64, offset=1024 * kib)
+            return shared.tile(shape, dtype, name=name, align_bytes=64, offset=int(1024 * kib))
 
         def bank(b, shape):
             return psum.tile(shape, F32, name="bank%d" % b, tag="bank%d" % b)
@@ -55,10 +56,12 @@ def tile_list_hoist_caution_scores_kernel(
         tabw = [slot((AREA_TAB0, AREA_TAB1)[a], [P, T], I32, "tabw%d" % a) for a in range(PASSES)]
         tabs = keep.tile([P, T], U8, name="tabs")
         ws_raw = keep.tile([P, 2, H], U8, name="ws_raw")
-        planes = keep.tile([P, PASSES, S + 2 * H], U8, name="planes", align_bytes=64)
+        planes = keep.tile([P, PASSES, S + 2 * P], U8, name="planes", align_bytes=64)
         nc.vector.memset(tabs[0:ROW0, :].bitcast(I32), 0)
         nc.vector.memset(ws_raw[0:ROW0, :, :].bitcast(I32), 0)
         nc.gpsimd.memset(planes[:].bitcast(I32), 0)
+        planes_rest = keep.tile([P, PASSES, (PACK - 1) * 2 * P], U8, name="planes_rest", align_bytes=64)
+        nc.gpsimd.memset(planes_rest[:].bitcast(I32), 0)
 
         nc.sync.dma_start(tabs[ROW0:P, :].bitcast(I32), tab_scales.rearrange("a q t -> q a t").bitcast(I32))
         nc.sync.dma_start(idx[:], offs)
@@ -78,12 +81,16 @@ def tile_list_hoist_caution_scores_kernel(
             nc.vector.tensor_copy(dst.rearrange("p a (t c i) -> p a c t i", t=PACK, i=run),
                                   src.rearrange("p a (c i t) -> p a c t i", t=PACK, i=run))
 
-        rows = slot(AREA_ROWS, [P, S + 2 * H], U8, "rows")
-        deal(rows[:, S:].rearrange("p (w c) -> p w c", w=2), ws_raw[:], 16)
+        def move_rows(dst, src):
+            for q in QUAD_ORDER:
+                nc.sync.dma_start(dst[32 * q : 32 * q + 4, :, :].bitcast(I32),
+                                  src[ROW0 + 8 * q : ROW0 + 8 * (q + 1), :].bitcast(I32))
+
+        rows = slot(AREA_ROWS, [P, S + 2 * P], U8, "rows")
+        ws_cols = ws_raw[:].rearrange("p w (c i t) -> p w c t i", t=PACK, i=16)
+        nc.vector.tensor_copy(rows[:, S:].rearrange("p (w c i) -> p w c i", w=2, i=16), ws_cols[:, :, :, 0, :])
         nc.vector.tensor_copy(rows[:, 0:S].bitcast(I32), vs_picked[:].bitcast(I32))
-        for q in range(QUADS):
-            nc.sync.dma_start(planes[32 * q : 32 * q + 4, :, :].bitcast(I32),
-                              rows[ROW0 + 8 * q : ROW0 + 8 * (q + 1), :].bitcast(I32))
+        move_rows(planes, rows)
         w2_raw = slot(AREA_W2, [P, PASSES, PACK, H], F32, "w2_raw")
         for a in range(PASSES):
             nc.sync.dma_start(w2_raw[:, a], w2[512 * a : 512 * (a + 1), :].rearrange("(p j) c -> p j c", j=PACK))
@@ -105,12 +112,12 @@ def tile_list_hoist_caution_scores_kernel(
         def load_wgs(part, kib):
             lo, hi = WGS_CUTS[part], WGS_CUTS[part + 1]
             dealt = slot(kib, [P, hi - lo], F32, "wgs%d" % part)
-            for q in (0, 2, 1, 3):
+            for q in QUAD_ORDER:
                 nc.sync.dma_start(dealt[32 * q : 32 * (q + 1), :], wgs_rows[:, lo:hi])
             for n in range(lo // BANK, hi // BANK):
                 wgs_parts[n] = dealt[:, BANK * n - lo : BANK * (n + 1) - lo]
 
-        load_wgs(0, AREA_ROWS - 1)
+        load_wgs(0, AREA_ROWS - 1.75)
         load_page(0, AREA_ROWS + 1)
 
         w1c = keep.tile([P, PASSES, 2 * H], U8, name="w1c", align_bytes=64)
@@ -121,25 +128,30 @@ def tile_list_hoist_caution_scores_kernel(
             nc.vector.tensor_copy(vw[1][:, BANK * u : BANK * (u + 1)],
                                   tabw[1][:].bitcast(U32).indirect(idx[:, LIST_COLS * u : LIST_COLS * (u + 1)]))
 
-        load_wgs(1, AREA_TAB1)
-        load_page(1, AREA_TAB1 + 6)
-        thr_sb = slot(AREA_TAB1 + 14, [P, PACK], F32, "thr_sb")
-        nc.sync.dma_start(thr_sb[:], thr.rearrange("(p t) -> p t", t=PACK))
-        gain_sb = slot(AREA_TAB1 + 15, [P, PACK], F32, "gain_sb")
-        nc.sync.dma_start(gain_sb[:], gain.rearrange("(p t) -> p t", t=PACK))
+        rows_rest = slot(AREA_ROWS + 0.25, [P, (PACK - 1) * 2 * P], U8, "rows_rest")
+        nc.vector.tensor_copy(rows_rest[:].rearrange("p (t w c i) -> p w c t i", w=2, t=PACK - 1, i=16),
+                              ws_cols[:, :, :, 1:PACK, :])
+        move_rows(planes_rest, rows_rest)
 
         w2_codes, w2_scales, w2_rest_bf = {}, {}, {}
         for a in range(PASSES):
-            first_bf = slot(AREA_FIRST + a, [P, P, PACK], BF16, "w2_first_bf%d" % a)
+            first_bf = slot((AREA_FIRST0, AREA_FIRST1)[a], [P, P, PACK], BF16, "w2_first_bf%d" % a)
             nc.vector.tensor_copy(first_bf[:], w2_raw[:, a].rearrange("p j (m t) -> p t m j", t=PACK)[:, 0, :, :])
             codes = keep.tile([P, P], U32, name="w2_first_codes%d" % a, align_bytes=64)
             scales = keep.tile([P, P], U8, name="w2_first_scales%d" % a, align_bytes=64)
             nc.vector.quantize_mx(out=codes[:].bitcast(FP8X4), scales=scales[:],
                                   in_=first_bf[:].rearrange("p m j -> p (m j)"))
             w2_codes[a, 0], w2_scales[a, 0] = codes[:], scales[:]
-        deal(w3c[:], w3_raw[:], 4)
-        load_page(2, AREA_TAB0 + 12)
-        load_wgs(2, AREA_FIRST)
+        load_wgs(1, AREA_FIRST0 - 5.75)
+        load_page(1, AREA_FIRST0 + 0.75)
+        thr_sb = slot(AREA_FIRST0 + 0.25, [P, PACK], F32, "thr_sb")
+        nc.sync.dma_start(thr_sb[:], thr.rearrange("(p t) -> p t", t=PACK))
+        gain_sb = slot(AREA_FIRST0 + 0.5, [P, PACK], F32, "gain_sb")
+        nc.sync.dma_start(gain_sb[:], gain.rearrange("(p t) -> p t", t=PACK))
+        w3_src = w3_raw[:].rearrange("p a (c i t) -> p a c t i", t=PACK, i=4)
+        w3_dst = w3c[:].rearrange("p a (t c i) -> p a c t i", t=PACK, i=4)
+        nc.vector.tensor_copy(w3_dst[:, :, :, 0, :], w3_src[:, :, :, 0, :])
+        load_wgs(2, AREA_FIRST1)
 
         def round_w2_rest(a):
             rest_bf = slot((AREA_REST0, AREA_REST1)[a], [P, PACK - 1, P, PACK], BF16, "w2_rest_bf%d" % a)
@@ -167,14 +179,20 @@ def tile_list_hoist_caution_scores_kernel(
                                     start=(a == 0), stop=(a == PASSES - 1))
             return acc
 
+        def weight_scales(w, a, t):
+            if t == 0:
+                return planes[:, a, S + P * w : S + P * (w + 1)]
+            lo = P * (2 * (t - 1) + w)
+            return planes_rest[:, a, lo : lo + P]
+
         def w1_operand(a, t):
-            return w1c[:, a, 2 * P * t : 2 * P * (t + 1)].bitcast(FP4X4), planes[:, a, S + P * t : S + P * (t + 1)]
+            return w1c[:, a, 2 * P * t : 2 * P * (t + 1)].bitcast(FP4X4), weight_scales(0, a, t)
 
         def w2_operand(a, t):
             return w2_codes[a, t].bitcast(FP8X4), w2_scales[a, t]
 
         def w3_operand(a, t):
-            return w3c[:, a, P * t : P * (t + 1)].bitcast(FP8X4), planes[:, a, S + H + P * t : S + H + P * (t + 1)]
+            return w3c[:, a, P * t : P * (t + 1)].bitcast(FP8X4), weight_scales(1, a, t)
 
         load_sb, wear, limit, worse = {}, {}, {}, {}
 
@@ -225,6 +243,8 @@ def tile_list_hoist_caution_scores_kernel(
             nc.vector.tensor_tensor(page[t][:].indirect(idx2[:, LIST_COLS * u : LIST_COLS * (u + 1)]),
                                     h[:], wgs_parts[n], ALU.mult)
             if n == 0:
+                nc.vector.tensor_copy(w3_dst[:, :, :, 1:PACK, :], w3_src[:, :, :, 1:PACK, :])
+                load_page(2, AREA_TAB0 + 12)
                 for a in range(PASSES):
                     quantise_w2_rest(a)
                 w4_raw = slot(AREA_REST0, [P, PACK, N], F32, "w4_raw")
@@ -240,7 +260,7 @@ def tile_list_hoist_caution_scores_kernel(
                 nc.scalar.copy(w4_bf[:].rearrange("p (c i) j -> p c j i", i=4),
                                w4_raw[:].rearrange("p j (c i) -> p c j i", i=4))
 
-        w4_codes = slot(AREA_FIRST + 6, [P, N], U32, "w4_codes")
+        w4_codes = slot(AREA_FIRST1 + 6, [P, N], U32, "w4_codes")
         w4_scales = keep.tile([P, N], U8, name="w4_scales", align_bytes=64)
         nc.vector.quantize_mx(out=w4_codes[:].bitcast(FP8X4), scales=w4_scales[:],
                               in_=w4_bf[:].rearrange("p n j -> p (n j)"))
@@ -253,9 +273,9 @@ def tile_list_hoist_caution_scores_kernel(
         def add_remarks(c):
             cols = slice(starts[c], starts[c + 1])
             y_bf[c] = keep.tile([P, WIDTHS[c], PACK], BF16, name="y_bf%d" % c, align_bytes=64)
-            nc.vector.tensor_tensor(y_bf[c][:].rearrange("p (c i) t -> p c t i", i=2),
-                                    gained[:, :, cols].rearrange("p t (c i) -> p c t i", i=2),
-                                    rem[:, :, cols].rearrange("p t (c i) -> p c t i", i=2), ALU.add)
+            nc.vector.tensor_tensor(y_bf[c][:].rearrange("p (c i) t -> p c t i", i=4),
+                                    gained[:, :, cols].rearrange("p t (c i) -> p c t i", i=4),
+                                    rem[:, :, cols].rearrange("p t (c i) -> p c t i", i=4), ALU.add)
 
         def finish(c):
             cols = slice(starts[c], starts[c + 1])

from contextlib import ExitStack

import concourse.mybir as mybir

K, T, S, T2, PM, H, N = 1024, 4096, 1024, 2048, 1024, 512, 512
FLOPS = 2 * (3 * K * H * S + H * N * PM)

F32 = mybir.dt.float32
BF16 = mybir.dt.bfloat16
I32 = mybir.dt.int32
U32 = mybir.dt.uint32
U16 = mybir.dt.uint16
U8 = mybir.dt.uint8
FP8X4 = mybir.dt.float8_e4m3fn_x4
FP4X4 = mybir.dt.float4_e2m1fn_x4
ALU = mybir.AluOpType
ACT = mybir.ActivationFunctionType

P = 128
PACK = 4
PASSES = K // (P * PACK)
QUADS = 4
BANK = 512
HALVES = S // BANK
STEPS = PACK * HALVES
LIST_COLS = BANK // 16
ROW0 = 96
QUAD_ORDER = (0, 2, 1, 3)
AREA_TAB0, AREA_TAB1, AREA_W2, AREA_ROWS, AREA_FIRST0, AREA_FIRST1, AREA_REST0, AREA_REST1 = 0, 20, 36, 54, 69, 78, 86, 94
WGS_CUTS = (0, BANK, 4 * BANK, 8 * BANK)
WIDTHS = (256, 256, 256, 128, 128)
GAIN_WIDTHS = (256, 512)


def tile_list_hoist_caution_scores_kernel(
    tc, tab_words, tab_scales, offs, offs2, offs3, w1_words, w1_scales, w2, w3_words, w3_scales,
    page0, wgs, thr, gain, remarks, w4, out,
):
    nc = tc.nc
    with ExitStack() as ctx:
        keep = ctx.enter_context(tc.tile_pool(name="keep", bufs=1))
        ring = ctx.enter_context(tc.tile_pool(name="ring", bufs=2))
        psum = ctx.enter_context(tc.psum_pool(name="psum", bufs=1))

        shared = ctx.enter_context(tc.tile_pool(name="shared", bufs=1))

        def slot(kib, shape, dtype, name):
            return shared.tile(shape, dtype, name=name, align_bytes=64, offset=int(1024 * kib))

        def bank(b, shape):
            return psum.tile(shape, F32, name="bank%d" % b, tag="bank%d" % b)

        idx = keep.tile([P, S // 16], U16, name="idx")
        idx2 = keep.tile([P, S // 16], U16, name="idx2")
        idx3 = keep.tile([P, PM // 16], U16, name="idx3")
        tabw = [slot((AREA_TAB0, AREA_TAB1)[a], [P, T], I32, "tabw%d" % a) for a in range(PASSES)]
        tabs = keep.tile([P, T], U8, name="tabs")
        ws_raw = keep.tile([P, 2, H], U8, name="ws_raw")
        planes = keep.tile([P, PASSES, S + 2 * P], U8, name="planes", align_bytes=64)
        nc.vector.memset(tabs[0:ROW0, :].bitcast(I32), 0)
        nc.vector.memset(ws_raw[0:ROW0, :, :].bitcast(I32), 0)
        nc.gpsimd.memset(planes[:].bitcast(I32), 0)
        planes_rest = keep.tile([P, PASSES, (PACK - 1) * 2 * P], U8, name="planes_rest", align_bytes=64)
        nc.gpsimd.memset(planes_rest[:].bitcast(I32), 0)

        nc.sync.dma_start(tabs[ROW0:P, :].bitcast(I32), tab_scales.rearrange("a q t -> q a t").bitcast(I32))
        nc.sync.dma_start(idx[:], offs)
        for w, scales in enumerate((w1_scales, w3_scales)):
            nc.sync.dma_start(ws_raw[ROW0:P, w, :].bitcast(I32), scales.rearrange("a q c -> q a c").bitcast(I32))
        nc.sync.dma_start(tabw[0][:], tab_words[0].rearrange("p t i -> p (t i)").bitcast(I32))
        nc.sync.dma_start(idx2[:], offs2)
        nc.sync.dma_start(idx3[:], offs3)
        w1_raw = keep.tile([P, PASSES, 2 * H], U8, name="w1_raw")
        nc.sync.dma_start(w1_raw[:].bitcast(I32), w1_words.rearrange("a p c -> p a c").bitcast(I32))
        nc.sync.dma_start(tabw[1][:], tab_words[1].rearrange("p t i -> p (t i)").bitcast(I32))

        vs_picked = slot(AREA_W2, [P, S], U8, "vs_picked")
        nc.vector.tensor_copy(vs_picked[:], tabs[:].indirect(idx[:]))

        def deal(dst, src, run):
            nc.vector.tensor_copy(dst.rearrange("p a (t c i) -> p a c t i", t=PACK, i=run),
                                  src.rearrange("p a (c i t) -> p a c t i", t=PACK, i=run))

        def move_rows(dst, src):
            for q in QUAD_ORDER:
                nc.sync.dma_start(dst[32 * q : 32 * q + 4, :, :].bitcast(I32),
                                  src[ROW0 + 8 * q : ROW0 + 8 * (q + 1), :].bitcast(I32))

        rows = slot(AREA_ROWS, [P, S + 2 * P], U8, "rows")
        ws_cols = ws_raw[:].rearrange("p w (c i t) -> p w c t i", t=PACK, i=16)
        nc.vector.tensor_copy(rows[:, S:].rearrange("p (w c i) -> p w c i", w=2, i=16), ws_cols[:, :, :, 0, :])
        nc.vector.tensor_copy(rows[:, 0:S].bitcast(I32), vs_picked[:].bitcast(I32))
        move_rows(planes, rows)
        w2_raw = slot(AREA_W2, [P, PASSES, PACK, H], F32, "w2_raw")
        for a in range(PASSES):
            nc.sync.dma_start(w2_raw[:, a], w2[512 * a : 512 * (a + 1), :].rearrange("(p j) c -> p j c", j=PACK))

        vw = [keep.tile([P, S], U32, name="vw%d" % a, align_bytes=64) for a in range(PASSES)]
        nc.vector.tensor_copy(vw[0][:], tabw[0][:].bitcast(U32).indirect(idx[:]))
        page_rows = page0.rearrange("(p t) c -> p t c", t=PACK)
        page = {}

        def load_page(t, kib):
            page[t] = slot(kib, [P, T2], F32, "page%d" % t)
            nc.sync.dma_start(page[t][:], page_rows[:, t, :])

        w3_raw = slot(AREA_TAB0 + 12, [P, PASSES, H], I32, "w3_raw")
        nc.sync.dma_start(w3_raw[:], w3_words.rearrange("a p c i -> p a (c i)").bitcast(I32))
        wgs_rows = wgs.rearrange("(q t) j -> q (t j)", t=PACK)
        wgs_parts = {}

        def load_wgs(part, kib):
            lo, hi = WGS_CUTS[part], WGS_CUTS[part + 1]
            dealt = slot(kib, [P, hi - lo], F32, "wgs%d" % part)
            for q in QUAD_ORDER:
                nc.sync.dma_start(dealt[32 * q : 32 * (q + 1), :], wgs_rows[:, lo:hi])
            for n in range(lo // BANK, hi // BANK):
                wgs_parts[n] = dealt[:, BANK * n - lo : BANK * (n + 1) - lo]

        load_wgs(0, AREA_ROWS - 1.75)
        load_page(0, AREA_ROWS + 1)

        w1c = keep.tile([P, PASSES, 2 * H], U8, name="w1c", align_bytes=64)
        w3c = keep.tile([P, PASSES, H], I32, name="w3c", align_bytes=64)
        deal(w1c[:].bitcast(U16), w1_raw[:].bitcast(U16), 8)

        for u in range(HALVES):
            nc.vector.tensor_copy(vw[1][:, BANK * u : BANK * (u + 1)],
                                  tabw[1][:].bitcast(U32).indirect(idx[:, LIST_COLS * u : LIST_COLS * (u + 1)]))

        rows_rest = slot(AREA_ROWS + 0.25, [P, (PACK - 1) * 2 * P], U8, "rows_rest")
        nc.vector.tensor_copy(rows_rest[:].rearrange("p (t w c i) -> p w c t i", w=2, t=PACK - 1, i=16),
                              ws_cols[:, :, :, 1:PACK, :])
        move_rows(planes_rest, rows_rest)

        w2_codes, w2_scales, w2_rest_bf = {}, {}, {}
        for a in range(PASSES):
            first_bf = slot((AREA_FIRST0, AREA_FIRST1)[a], [P, P, PACK], BF16, "w2_first_bf%d" % a)
            nc.vector.tensor_copy(first_bf[:], w2_raw[:, a].rearrange("p j (m t) -> p t m j", t=PACK)[:, 0, :, :])
            codes = keep.tile([P, P], U32, name="w2_first_codes%d" % a, align_bytes=64)
            scales = keep.tile([P, P], U8, name="w2_first_scales%d" % a, align_bytes=64)
            nc.vector.quantize_mx(out=codes[:].bitcast(FP8X4), scales=scales[:],
                                  in_=first_bf[:].rearrange("p m j -> p (m j)"))
            w2_codes[a, 0], w2_scales[a, 0] = codes[:], scales[:]
        load_wgs(1, AREA_FIRST0 - 5.75)
        load_page(1, AREA_FIRST0 + 0.75)
        thr_sb = slot(AREA_FIRST0 + 0.25, [P, PACK], F32, "thr_sb")
        nc.sync.dma_start(thr_sb[:], thr.rearrange("(p t) -> p t", t=PACK))
        gain_sb = slot(AREA_FIRST0 + 0.5, [P, PACK], F32, "gain_sb")
        nc.sync.dma_start(gain_sb[:], gain.rearrange("(p t) -> p t", t=PACK))
        w3_src = w3_raw[:].rearrange("p a (c i t) -> p a c t i", t=PACK, i=4)
        w3_dst = w3c[:].rearrange("p a (t c i) -> p a c t i", t=PACK, i=4)
        nc.vector.tensor_copy(w3_dst[:, :, :, 0, :], w3_src[:, :, :, 0, :])
        load_wgs(2, AREA_FIRST1)

        def round_w2_rest(a):
            rest_bf = slot((AREA_REST0, AREA_REST1)[a], [P, PACK - 1, P, PACK], BF16, "w2_rest_bf%d" % a)
            nc.scalar.copy(rest_bf[:].rearrange("p t m j -> p m j t"),
                           w2_raw[:, a].rearrange("p j (m t) -> p m j t", t=PACK)[:, :, :, 1:PACK])
            w2_rest_bf[a] = rest_bf

        def quantise_w2_rest(a):
            codes = keep.tile([P, (PACK - 1) * P], U32, name="w2_rest_codes%d" % a, align_bytes=64)
            scales = keep.tile([P, (PACK - 1) * P], U8, name="w2_rest_scales%d" % a, align_bytes=64)
            nc.vector.quantize_mx(out=codes[:].bitcast(FP8X4), scales=scales[:],
                                  in_=w2_rest_bf[a][:].rearrange("p t m j -> p (t m j)"))
            for t in range(1, PACK):
                w2_codes[a, t] = codes[:, P * (t - 1) : P * t]
                w2_scales[a, t] = scales[:, P * (t - 1) : P * t]

        def product(b, n, operand):
            t, u = divmod(n, HALVES)
            cols = slice(BANK * u, BANK * (u + 1))
            acc = bank(b, [P, BANK])
            for a in range(PASSES):
                codes, scales = operand(a, t)
                nc.tensor.matmul_mx(out=acc[:], lhsT=codes, lhsT_scale=scales,
                                    rhs=vw[a][:, cols].bitcast(FP8X4), rhs_scale=planes[:, a, cols],
                                    start=(a == 0), stop=(a == PASSES - 1))
            return acc

        def weight_scales(w, a, t):
            if t == 0:
                return planes[:, a, S + P * w : S + P * (w + 1)]
            lo = P * (2 * (t - 1) + w)
            return planes_rest[:, a, lo : lo + P]

        def w1_operand(a, t):
            return w1c[:, a, 2 * P * t : 2 * P * (t + 1)].bitcast(FP4X4), weight_scales(0, a, t)

        def w2_operand(a, t):
            return w2_codes[a, t].bitcast(FP8X4), w2_scales[a, t]

        def w3_operand(a, t):
            return w3c[:, a, P * t : P * (t + 1)].bitcast(FP8X4), weight_scales(1, a, t)

        load_sb, wear, limit, worse = {}, {}, {}, {}

        def load_product(n):
            acc = product(n % 2, n, w1_operand)
            load_sb[n] = ring.tile([P, BANK], F32, name="load_sb", tag="load_sb", bufs=STEPS)
            nc.scalar.copy(load_sb[n][:], acc[:])

        def limit_product(n):
            limit[n] = product(5 + n % 3, n, w3_operand)

        def wear_product(n):
            wear[n] = product(2 + n % 3, n, w2_operand)

        def take_max(n):
            worse[n] = ring.tile([P, BANK], F32, name="worse", tag="worse")
            nc.vector.tensor_tensor(worse[n][:], wear[n][:], load_sb[n][:], ALU.max)

        gained = keep.tile([P, PACK, PM], F32, name="gained")

        def look(t, lo, hi):
            looked = keep.tile([P, hi - lo], F32, name="looked", tag="looked")
            nc.scalar.activation(out=looked[:], in_=page[t][:].indirect(idx3[:, lo // 16 : hi // 16]),
                                 func=ACT.Sigmoid, bias=thr_sb[:, t : t + 1])
            return looked

        def apply_gain(t, looked, base, lo, hi):
            nc.scalar.activation(out=gained[:, t, lo:hi], in_=looked[:, lo - base : hi - base], func=ACT.Copy,
                                 scale=gain_sb[:, t : t + 1])

        round_w2_rest(0)
        for n in range(2):
            load_product(n)
        for n in range(2):
            wear_product(n)
            limit_product(n)
        round_w2_rest(1)
        rem = slot(AREA_W2, [P, PACK, PM], F32, "rem")
        nc.sync.dma_start(rem[:], remarks.rearrange("(p t) m -> p t m", t=PACK))
        take_max(0)
        w4_bf = keep.tile([P, N, PACK], BF16, name="w4_bf", align_bytes=64)
        for n in range(STEPS):
            t, u = divmod(n, HALVES)
            h = ring.tile([P, BANK], F32, name="h", tag="h")
            nc.vector.tensor_tensor(h[:], limit[n][:], worse[n][:], ALU.min)
            if n + 1 < STEPS:
                take_max(n + 1)
            nc.vector.tensor_tensor(page[t][:].indirect(idx2[:, LIST_COLS * u : LIST_COLS * (u + 1)]),
                                    h[:], wgs_parts[n], ALU.mult)
            if n == 0:
                nc.vector.tensor_copy(w3_dst[:, :, :, 1:PACK, :], w3_src[:, :, :, 1:PACK, :])
                load_page(2, AREA_TAB0 + 12)
                for a in range(PASSES):
                    quantise_w2_rest(a)
                w4_raw = slot(AREA_REST0, [P, PACK, N], F32, "w4_raw")
                nc.sync.dma_start(w4_raw[:], w4.rearrange("(p j) n -> p j n", j=PACK))
                load_page(3, AREA_REST1)
            if n + 2 < STEPS:
                load_product(n + 2)
                wear_product(n + 2)
                limit_product(n + 2)
            if u == HALVES - 1 and t < PACK - 1:
                apply_gain(t, look(t, 0, PM), 0, 0, PM)
            if n == STEPS - 3:
                nc.scalar.copy(w4_bf[:].rearrange("p (c i) j -> p c j i", i=4),
                               w4_raw[:].rearrange("p j (c i) -> p c j i", i=4))

        w4_codes = slot(AREA_FIRST1 + 6, [P, N], U32, "w4_codes")
        w4_scales = keep.tile([P, N], U8, name="w4_scales", align_bytes=64)
        nc.vector.quantize_mx(out=w4_codes[:].bitcast(FP8X4), scales=w4_scales[:],
                              in_=w4_bf[:].rearrange("p n j -> p (n j)"))

        chunks = len(WIDTHS)
        starts = [sum(WIDTHS[:c]) for c in range(chunks + 1)]
        out_rows = out.rearrange("(b p) m -> p b m", p=P)
        y_bf = {}

        def add_remarks(c):
            cols = slice(starts[c], starts[c + 1])
            y_bf[c] = keep.tile([P, WIDTHS[c], PACK], BF16, name="y_bf%d" % c, align_bytes=64)
            nc.vector.tensor_tensor(y_bf[c][:].rearrange("p (c i) t -> p c t i", i=4),
                                    gained[:, :, cols].rearrange("p t (c i) -> p c t i", i=4),
                                    rem[:, :, cols].rearrange("p t (c i) -> p c t i", i=4), ALU.add)

        def finish(c):
            cols = slice(starts[c], starts[c + 1])
            width = WIDTHS[c]
            codes = keep.tile([P, width], U32, name="y_codes%d" % c, align_bytes=64)
            scales = keep.tile([P, width], U8, name="y_scales%d" % c, align_bytes=64)
            nc.vector.quantize_mx(out=codes[:].bitcast(FP8X4), scales=scales[:],
                                  in_=y_bf[c][:].rearrange("p m t -> p (m t)"))
            for g in range(2):
                acc = bank((2 * c + g) % 8, [P, 2, width])
                for e in range(2):
                    ncols = slice(P * (2 * g + e), P * (2 * g + e + 1))
                    nc.tensor.matmul_mx(out=acc[:, e, :], lhsT=w4_codes[:, ncols].bitcast(FP8X4),
                                        lhsT_scale=w4_scales[:, ncols], rhs=codes[:].bitcast(FP8X4),
                                        rhs_scale=scales[:], start=True, stop=True)
                staged = keep.tile([P, 2, width], F32, name="staged%d_%d" % (c, g))
                if c >= chunks - 2 and g == 1:
                    nc.vector.tensor_copy(staged[:], acc[:])
                else:
                    nc.scalar.copy(staged[:], acc[:])
                queue = nc.scalar if (c, g) == (chunks - 1, 0) else nc.sync
                queue.dma_start(out_rows[:, 2 * g : 2 * g + 2, cols], staged[:])

        last = PACK - 1
        for u in range(HALVES):
            looked = look(last, BANK * u, BANK * (u + 1))
            for lo in range(BANK * u, BANK * (u + 1), GAIN_WIDTHS[u]):
                apply_gain(last, looked, BANK * u, lo, lo + GAIN_WIDTHS[u])
        for c in range(chunks):
            add_remarks(c)
            if c > 0:
                finish(c - 1)
        finish(chunks - 1)
